import numpy as np
import ml_dtypes


def mxq(x, axis, fmt="e4m3"):
    dtype, down = {"e4m3": (ml_dtypes.float8_e4m3fn, 7), "e5m2": (ml_dtypes.float8_e5m2, 14)}[fmt]
    v = np.moveaxis(np.asarray(x, np.float32).astype(ml_dtypes.bfloat16).astype(np.float64), axis, -1)
    blocks = v.reshape(v.shape[:-1] + (-1, 32))
    amax = np.abs(blocks).max(-1, keepdims=True)
    byte = np.maximum(np.where(amax > 0, np.frexp(amax)[1] - 1 + 127, 0) - down, 1)
    scale = np.exp2(byte - 127.0)
    codes = (blocks / scale).astype(np.float32).astype(dtype).astype(np.float64)
    return np.moveaxis((codes * scale).reshape(v.shape), -1, axis)


WIDE = False


def mx_kscale(k):
    if not WIDE:
        return np.ones(k)
    levels = np.array([10, -10, 5, -5, 0])
    if k % 512:
        return np.exp2(np.random.permutation(np.resize(levels, k // 32))).repeat(32)
    a = np.empty((k // 512, 16))
    for p in range(k // 512):
        a[p, :8] = np.random.permutation(np.resize(levels, 8))
        for g in range(8):
            far = levels[np.abs(levels - a[p, g]) >= 10]
            a[p, g + 8] = far[np.random.randint(len(far))]
    return np.exp2(a.ravel()).repeat(32)


def f64(x):
    return np.asarray(x).astype(np.float64)


def striped(idx):
    return np.tile(idx.reshape(-1, 16).T, (8, 1)).astype(np.uint16)


def unstriped(offs):
    return offs[:16].T.reshape(-1).astype(np.int64)


def pack_weight(w):
    k, n = w.shape
    w = f64(np.asarray(w, np.float32).astype(ml_dtypes.bfloat16)).reshape(k // 32, 32, n)
    amax = np.abs(w).max(1)
    byte = np.clip(np.where(amax > 0, np.frexp(amax)[1] - 1 + 127 - 7, 1), 1, 254)
    scaled = (w * np.exp2(127.0 - byte)[:, None, :]).reshape(k, n).astype(np.float32)
    words = np.ascontiguousarray(scaled.reshape(k // 512, 128, 4, n).transpose(0, 1, 3, 2)).astype(ml_dtypes.float8_e4m3fn).view(np.uint8)
    return words, np.ascontiguousarray(byte.astype(np.uint8).reshape(k // 512, 16, n))


def unpack_weight(words, scales):
    g, p, n, _ = words.shape
    vals = np.ascontiguousarray(words).view(ml_dtypes.float8_e4m3fn).astype(np.float64) * np.repeat(np.exp2(scales.astype(np.float64) - 127.0), 8, axis=1)[..., None]
    return vals.transpose(0, 1, 3, 2).reshape(g * 512, n)


K, T, D, S, V, N = 2048, 1024, 4, 512, 128, 128


def setup_inputs():
    n = np.random.standard_normal
    s = mx_kscale(K)[:, None]
    words, scales = pack_weight(n((K, N)) / np.sqrt(K) / s)
    return {
        "xT": (n((K, T)) * s).astype(np.float32),
        "w_words": words,
        "w_scales": scales,
        "b": (0.3 * n((N, 1))).astype(np.float32),
        "offs": striped(np.random.permutation(T)[:S]),
    }


def reference(xT, w_words, w_scales, b, offs):
    w = unpack_weight(w_words, w_scales)
    idx = unstriped(offs)
    xq = mxq(f64(xT)[:, idx], 0, "e4m3")
    y = w.T @ xq
    y = y + f64(b)
    return y.reshape(N, V, D).max(axis=2)

@@ -1,0 +1,105 @@
+from contextlib import ExitStack
+
+import concourse.mybir as mybir
+
+K, T, D, S, V, N = 2048, 1024, 4, 512, 128, 128
+FLOPS = 2 * K * N * S
+
+F32 = mybir.dt.float32
+BF16 = mybir.dt.bfloat16
+I32 = mybir.dt.int32
+U32 = mybir.dt.uint32
+U16 = mybir.dt.uint16
+U8 = mybir.dt.uint8
+FP8X4 = mybir.dt.float8_e4m3fn_x4
+
+P = 128
+PACK = 4
+K_PASS = P * PACK
+PASSES = K // K_PASS
+HALF = S // 2
+CHUNKS = [[(0, 512), (512, 1024)]] * 8
+VECTOR_SHARE = {(0, 1): 352, (7, 1): 352}
+
+
+def tile_picked_pool_lin_bias_sub_e_kernel(tc, xT, w_words, w_scales, b, offs, out):
+    nc = tc.nc
+    with ExitStack() as ctx:
+        keep = ctx.enter_context(tc.tile_pool(name="keep", bufs=1))
+        psum = ctx.enter_context(tc.psum_pool(name="psum", bufs=1))
+
+        offsets = keep.tile([P, S // 16], U16, name="offsets")
+        w_codes = keep.tile([P, PASSES, N], U32, name="w_codes", align_bytes=64)
+        w_plane = keep.tile([P, N], U8, name="w_plane", align_bytes=64)
+        bias = keep.tile([P, 1], F32, name="bias")
+        nc.vector.memset(w_plane[:].bitcast(I32), 0)
+
+        x_rows = xT.rearrange("(a p j) t -> a p j t", p=P, j=PACK)
+        raw = {}
+        for i in range(2 * PASSES):
+            a, u = divmod(i, 2)
+            for c, (t0, t1) in enumerate(CHUNKS[i]):
+                raw[i, c] = keep.tile([P, 2, t1 - t0], F32, name="raw_%d_%d" % (i, c))
+                nc.sync.dma_start(raw[i, c][:], x_rows[a, :, 2 * u : 2 * u + 2, t0:t1])
+                if (i, c) == (0, 0):
+                    nc.sync.dma_start(offsets[:], offs)
+        scale_words = w_scales.bitcast(I32)
+        for q in range(4):
+            nc.sync.dma_start(w_plane[32 * q : 32 * q + 16, :].bitcast(I32), scale_words[:, 4 * q : 4 * q + 4, :])
+        nc.sync.dma_start(w_codes[:].bitcast(I32), w_words.rearrange("a p m r -> p a (m r)").bitcast(I32))
+        nc.sync.dma_start(bias[:], b)
+
+        acc = [psum.tile([P, HALF], F32, name="acc_%d" % h) for h in range(2)]
+        pooled = keep.tile([P, V], F32, name="pooled")
+        result = keep.tile([P, V], F32, name="result")
+
+        def cast(i):
+            pairs = keep.tile([P, T, 2], BF16, name="pairs_%d" % i)
+            for c, (t0, t1) in enumerate(CHUNKS[i]):
+                src = raw[i, c][:].rearrange("p j t -> p t j")
+                cut = t1 - t0 - VECTOR_SHARE.get((i, c), 0)
+                nc.scalar.copy(pairs[:, t0 : t0 + cut, :], src[:, :cut, :])
+                if cut < t1 - t0:
+                    nc.vector.tensor_copy(pairs[:, t0 + cut : t1, :], src[:, cut:, :])
+            return pairs[:].rearrange("p t j -> p (t j)").bitcast(U32)
+
+        for a in range(PASSES):
+            grouped = keep.tile([P, PACK * S], BF16, name="grouped_%d" % a, align_bytes=64)
+            codes = keep.tile([P, S], U32, name="codes_%d" % a, align_bytes=64)
+            plane = keep.tile([P, S], U8, name="plane_%d" % a, align_bytes=64)
+            last = a == PASSES - 1
+            parts = [(0, HALF), (HALF, S)]
+            for u in range(2):
+                window = cast(2 * a + u)
+                for j0, j1 in parts if u == 1 else [(0, S)]:
+                    nc.vector.tensor_copy(
+                        grouped[:].bitcast(U32)[:, 2 * j0 + u : 2 * j1 : 2],
+                        window.indirect(offsets[:, j0 // 16 : j1 // 16]),
+                    )
+            for j0, j1 in parts:
+                nc.vector.quantize_mx(
+                    out=codes[:, j0:j1].bitcast(FP8X4),
+                    scales=plane[:, j0:j1],
+                    in_=grouped[:, PACK * j0 : PACK * j1],
+                )
+            for h in range(2):
+                cols = slice(h * HALF, (h + 1) * HALF)
+                nc.tensor.matmul_mx(
+                    out=acc[h][:],
+                    lhsT=w_codes[:, a, :].bitcast(FP8X4),
+                    lhsT_scale=w_plane[4 * a :, :],
+                    rhs=codes[:, cols].bitcast(FP8X4),
+                    rhs_scale=plane[:, cols],
+                    start=(a == 0),
+                    stop=last,
+                )
+
+        for h in range(2):
+            nc.vector.tensor_reduce(
+                pooled[:, h * V // 2 : (h + 1) * V // 2],
+                acc[h][:].rearrange("p (v d) -> p v d", d=D),
+                mybir.AxisListType.X,
+                mybir.AluOpType.max,
+            )
+        nc.vector.tensor_scalar_add(result[:], pooled[:], bias[:])
+        nc.sync.dma_start(out, result[:])

@@ -17,9 +17,14 @@ P = 128
 PACK = 4
 K_PASS = P * PACK
 PASSES = K // K_PASS
-HALF = S // 2
-CHUNKS = [[(0, 512), (512, 1024)]] * 8
-VECTOR_SHARE = {(0, 1): 352, (7, 1): 352}
+WHOLE = [(0, T)]
+HALVES = [(0, T // 2), (T // 2, T)]
+CHUNKS = [WHOLE] * 4 + [HALVES] * 4
+VECTOR_SHARE = {(0, 0): 632, (1, 0): 616, (2, 0): 152, (3, 0): 320, (4, 0): 168, (4, 1): 168, (5, 0): 112, (7, 1): 216}
+GATHERS = [(0, 128), (128, 256), (256, 384), (384, 512)]
+GROUPS = [(0, 256), (256, 512)]
+QUANTS = [(0, 256), (256, 384), (384, 512)]
+EARLY = [(0, 256), (256, 512)]
 
 
 def tile_picked_pool_lin_bias_sub_e_kernel(tc, xT, w_words, w_scales, b, offs, out):
@@ -34,6 +39,10 @@ def tile_picked_pool_lin_bias_sub_e_kernel(tc, xT, w_words, w_scales, b, offs, o
         bias = keep.tile([P, 1], F32, name="bias")
         nc.vector.memset(w_plane[:].bitcast(I32), 0)
 
+        scale_words = w_scales.bitcast(I32)
+        for q in range(4):
+            nc.scalar.dma_start(w_plane[32 * q : 32 * q + 16, :].bitcast(I32), scale_words[:, 4 * q : 4 * q + 4, :])
+
         x_rows = xT.rearrange("(a p j) t -> a p j t", p=P, j=PACK)
         raw = {}
         for i in range(2 * PASSES):
@@ -43,13 +52,9 @@ def tile_picked_pool_lin_bias_sub_e_kernel(tc, xT, w_words, w_scales, b, offs, o
                 nc.sync.dma_start(raw[i, c][:], x_rows[a, :, 2 * u : 2 * u + 2, t0:t1])
                 if (i, c) == (0, 0):
                     nc.sync.dma_start(offsets[:], offs)
-        scale_words = w_scales.bitcast(I32)
-        for q in range(4):
-            nc.sync.dma_start(w_plane[32 * q : 32 * q + 16, :].bitcast(I32), scale_words[:, 4 * q : 4 * q + 4, :])
         nc.sync.dma_start(w_codes[:].bitcast(I32), w_words.rearrange("a p m r -> p a (m r)").bitcast(I32))
         nc.sync.dma_start(bias[:], b)
 
-        acc = [psum.tile([P, HALF], F32, name="acc_%d" % h) for h in range(2)]
         pooled = keep.tile([P, V], F32, name="pooled")
         result = keep.tile([P, V], F32, name="result")
 
@@ -63,41 +68,48 @@ def tile_picked_pool_lin_bias_sub_e_kernel(tc, xT, w_words, w_scales, b, offs, o
                     nc.vector.tensor_copy(pairs[:, t0 + cut : t1, :], src[:, cut:, :])
             return pairs[:].rearrange("p t j -> p (t j)").bitcast(U32)
 
+        codes, planes = [], []
         for a in range(PASSES):
+            picked = keep.tile([P, 2, 2 * S], BF16, name="picked_%d" % a)
             grouped = keep.tile([P, PACK * S], BF16, name="grouped_%d" % a, align_bytes=64)
-            codes = keep.tile([P, S], U32, name="codes_%d" % a, align_bytes=64)
-            plane = keep.tile([P, S], U8, name="plane_%d" % a, align_bytes=64)
+            codes.append(keep.tile([P, S], U32, name="codes_%d" % a, align_bytes=64))
+            planes.append(keep.tile([P, S], U8, name="plane_%d" % a, align_bytes=64))
             last = a == PASSES - 1
-            parts = [(0, HALF), (HALF, S)]
             for u in range(2):
                 window = cast(2 * a + u)
-                for j0, j1 in parts if u == 1 else [(0, S)]:
+                for j0, j1 in (GATHERS if last else EARLY) if u == 1 else [(0, S)]:
                     nc.vector.tensor_copy(
-                        grouped[:].bitcast(U32)[:, 2 * j0 + u : 2 * j1 : 2],
+                        picked[:, u, 2 * j0 : 2 * j1].bitcast(U32),
                         window.indirect(offsets[:, j0 // 16 : j1 // 16]),
                     )
-            for j0, j1 in parts:
+            for j0, j1 in GATHERS if last else EARLY:
+                copy = nc.scalar.copy if last else nc.vector.tensor_copy
+                copy(
+                    grouped[:, PACK * j0 : PACK * j1].bitcast(F32).rearrange("p (n u) -> p n u", u=2),
+                    picked[:, :, 2 * j0 : 2 * j1].bitcast(F32).rearrange("p u n -> p n u"),
+                )
+            for j0, j1 in QUANTS if last else EARLY:
                 nc.vector.quantize_mx(
-                    out=codes[:, j0:j1].bitcast(FP8X4),
-                    scales=plane[:, j0:j1],
+                    out=codes[a][:, j0:j1].bitcast(FP8X4),
+                    scales=planes[a][:, j0:j1],
                     in_=grouped[:, PACK * j0 : PACK * j1],
                 )
-            for h in range(2):
-                cols = slice(h * HALF, (h + 1) * HALF)
+
+        for h, (j0, j1) in enumerate(GROUPS):
+            acc = psum.tile([P, j1 - j0], F32, name="acc_%d" % h)
+            for a in range(PASSES):
                 nc.tensor.matmul_mx(
-                    out=acc[h][:],
+                    out=acc[:],
                     lhsT=w_codes[:, a, :].bitcast(FP8X4),
                     lhsT_scale=w_plane[4 * a :, :],
-                    rhs=codes[:, cols].bitcast(FP8X4),
-                    rhs_scale=plane[:, cols],
+                    rhs=codes[a][:, j0:j1].bitcast(FP8X4),
+                    rhs_scale=planes[a][:, j0:j1],
                     start=(a == 0),
-                    stop=last,
+                    stop=(a == PASSES - 1),
                 )
-
-        for h in range(2):
             nc.vector.tensor_reduce(
-                pooled[:, h * V // 2 : (h + 1) * V // 2],
-                acc[h][:].rearrange("p (v d) -> p v d", d=D),
+                pooled[:, j0 // D : j1 // D],
+                acc[:].rearrange("p (v d) -> p v d", d=D),
                 mybir.AxisListType.X,
                 mybir.AluOpType.max,
             )

@@ -17,14 +17,14 @@ P = 128
 PACK = 4
 K_PASS = P * PACK
 PASSES = K // K_PASS
-WHOLE = [(0, T)]
-HALVES = [(0, T // 2), (T // 2, T)]
-CHUNKS = [WHOLE] * 4 + [HALVES] * 4
-VECTOR_SHARE = {(0, 0): 632, (1, 0): 616, (2, 0): 152, (3, 0): 320, (4, 0): 168, (4, 1): 168, (5, 0): 112, (7, 1): 216}
-GATHERS = [(0, 128), (128, 256), (256, 384), (384, 512)]
-GROUPS = [(0, 256), (256, 512)]
-QUANTS = [(0, 256), (256, 384), (384, 512)]
+PAIRS = 2 * PASSES
+WHOLE = [(0, T, 608)]
+HALVES = [(0, 512, 128), (512, T, 0)]
+LAST = [(0, 256, 256), (256, 576, 0), (576, 832, 0), (832, T, 0)]
+CHUNKS = [WHOLE] * 2 + [HALVES] * 4 + [[(0, 512, 0), (512, T, 0)], LAST]
 EARLY = [(0, 256), (256, 512)]
+QUARTERS = [(0, 128), (128, 256), (256, 384), (384, 512)]
+GROUPS = [(0, 256), (256, 384), (384, 512)]
 
 
 def tile_picked_pool_lin_bias_sub_e_kernel(tc, xT, w_words, w_scales, b, offs, out):
@@ -45,9 +45,9 @@ def tile_picked_pool_lin_bias_sub_e_kernel(tc, xT, w_words, w_scales, b, offs, o
 
         x_rows = xT.rearrange("(a p j) t -> a p j t", p=P, j=PACK)
         raw = {}
-        for i in range(2 * PASSES):
+        for i in range(PAIRS):
             a, u = divmod(i, 2)
-            for c, (t0, t1) in enumerate(CHUNKS[i]):
+            for c, (t0, t1, share) in enumerate(CHUNKS[i]):
                 raw[i, c] = keep.tile([P, 2, t1 - t0], F32, name="raw_%d_%d" % (i, c))
                 nc.sync.dma_start(raw[i, c][:], x_rows[a, :, 2 * u : 2 * u + 2, t0:t1])
                 if (i, c) == (0, 0):
@@ -57,59 +57,81 @@ def tile_picked_pool_lin_bias_sub_e_kernel(tc, xT, w_words, w_scales, b, offs, o
 
         pooled = keep.tile([P, V], F32, name="pooled")
         result = keep.tile([P, V], F32, name="result")
+        picked = [keep.tile([P, 2, 2 * S], BF16, name="picked_%d" % a) for a in range(PASSES)]
+        grouped = [keep.tile([P, PACK * S], BF16, name="grouped_%d" % a, align_bytes=64) for a in range(PASSES)]
+        codes = [keep.tile([P, S], U32, name="codes_%d" % a, align_bytes=64) for a in range(PASSES)]
+        planes = [keep.tile([P, S], U8, name="plane_%d" % a, align_bytes=64) for a in range(PASSES)]
+        accs = [psum.tile([P, j1 - j0], F32, name="acc_%d" % j0) for j0, j1 in GROUPS]
 
-        def cast(i):
+        def round_pair(i):
             pairs = keep.tile([P, T, 2], BF16, name="pairs_%d" % i)
-            for c, (t0, t1) in enumerate(CHUNKS[i]):
+            for c, (t0, t1, share) in enumerate(CHUNKS[i]):
                 src = raw[i, c][:].rearrange("p j t -> p t j")
-                cut = t1 - t0 - VECTOR_SHARE.get((i, c), 0)
-                nc.scalar.copy(pairs[:, t0 : t0 + cut, :], src[:, :cut, :])
-                if cut < t1 - t0:
+                cut = t1 - t0 - share
+                if cut > 0:
+                    nc.scalar.copy(pairs[:, t0 : t0 + cut, :], src[:, :cut, :])
+                if share > 0:
                     nc.vector.tensor_copy(pairs[:, t0 + cut : t1, :], src[:, cut:, :])
             return pairs[:].rearrange("p t j -> p (t j)").bitcast(U32)
 
-        codes, planes = [], []
-        for a in range(PASSES):
-            picked = keep.tile([P, 2, 2 * S], BF16, name="picked_%d" % a)
-            grouped = keep.tile([P, PACK * S], BF16, name="grouped_%d" % a, align_bytes=64)
-            codes.append(keep.tile([P, S], U32, name="codes_%d" % a, align_bytes=64))
-            planes.append(keep.tile([P, S], U8, name="plane_%d" % a, align_bytes=64))
-            last = a == PASSES - 1
-            for u in range(2):
-                window = cast(2 * a + u)
-                for j0, j1 in (GATHERS if last else EARLY) if u == 1 else [(0, S)]:
-                    nc.vector.tensor_copy(
-                        picked[:, u, 2 * j0 : 2 * j1].bitcast(U32),
-                        window.indirect(offsets[:, j0 // 16 : j1 // 16]),
-                    )
-            for j0, j1 in GATHERS if last else EARLY:
-                copy = nc.scalar.copy if last else nc.vector.tensor_copy
-                copy(
-                    grouped[:, PACK * j0 : PACK * j1].bitcast(F32).rearrange("p (n u) -> p n u", u=2),
-                    picked[:, :, 2 * j0 : 2 * j1].bitcast(F32).rearrange("p u n -> p n u"),
-                )
-            for j0, j1 in QUANTS if last else EARLY:
-                nc.vector.quantize_mx(
-                    out=codes[a][:, j0:j1].bitcast(FP8X4),
-                    scales=planes[a][:, j0:j1],
-                    in_=grouped[:, PACK * j0 : PACK * j1],
-                )
+        def gather(i, window, j0, j1):
+            a, u = divmod(i, 2)
+            nc.vector.tensor_copy(
+                picked[a][:, u, 2 * j0 : 2 * j1].bitcast(U32),
+                window.indirect(offsets[:, j0 // 16 : j1 // 16]),
+            )
 
-        for h, (j0, j1) in enumerate(GROUPS):
-            acc = psum.tile([P, j1 - j0], F32, name="acc_%d" % h)
-            for a in range(PASSES):
-                nc.tensor.matmul_mx(
-                    out=acc[:],
-                    lhsT=w_codes[:, a, :].bitcast(FP8X4),
-                    lhsT_scale=w_plane[4 * a :, :],
-                    rhs=codes[a][:, j0:j1].bitcast(FP8X4),
-                    rhs_scale=planes[a][:, j0:j1],
-                    start=(a == 0),
-                    stop=(a == PASSES - 1),
-                )
+        def weave(copy, a, j0, j1):
+            copy(
+                grouped[a][:, PACK * j0 : PACK * j1].bitcast(F32).rearrange("p (n u) -> p n u", u=2),
+                picked[a][:, :, 2 * j0 : 2 * j1].bitcast(F32).rearrange("p u n -> p n u"),
+            )
+
+        def quantise(a, j0, j1):
+            nc.vector.quantize_mx(
+                out=codes[a][:, j0:j1].bitcast(FP8X4),
+                scales=planes[a][:, j0:j1],
+                in_=grouped[a][:, PACK * j0 : PACK * j1],
+            )
+
+        def multiply(a, g):
+            j0, j1 = GROUPS[g]
+            nc.tensor.matmul_mx(
+                out=accs[g][:],
+                lhsT=w_codes[:, a, :].bitcast(FP8X4),
+                lhsT_scale=w_plane[4 * a :, :],
+                rhs=codes[a][:, j0:j1].bitcast(FP8X4),
+                rhs_scale=planes[a][:, j0:j1],
+                start=(a == 0),
+                stop=(a == PASSES - 1),
+            )
+
+        last = PASSES - 1
+        gather(0, round_pair(0), 0, S)
+        window = round_pair(1)
+        for a in range(last):
+            for j0, j1 in EARLY:
+                gather(2 * a + 1, window, j0, j1)
+            for j0, j1 in EARLY:
+                weave(nc.vector.tensor_copy, a, j0, j1)
+            for j0, j1 in EARLY:
+                quantise(a, j0, j1)
+            gather(2 * a + 2, round_pair(2 * a + 2), 0, S)
+            window = round_pair(2 * a + 3)
+        for j0, j1 in QUARTERS:
+            gather(2 * last + 1, window, j0, j1)
+        for g in range(len(GROUPS)):
+            for a in range(last):
+                multiply(a, g)
+        for j0, j1 in QUARTERS:
+            weave(nc.scalar.copy, last, j0, j1)
+        for g, (j0, j1) in enumerate(GROUPS):
+            quantise(last, j0, j1)
+            multiply(last, g)
+        for g, (j0, j1) in enumerate(GROUPS):
             nc.vector.tensor_reduce(
                 pooled[:, j0 // D : j1 // D],
-                acc[:].rearrange("p (v d) -> p v d", d=D),
+                accs[g][:].rearrange("p (v d) -> p v d", d=D),
                 mybir.AxisListType.X,
                 mybir.AluOpType.max,
             )

@@ -19,9 +19,9 @@ K_PASS = P * PACK
 PASSES = K // K_PASS
 PAIRS = 2 * PASSES
 WHOLE = [(0, T, 608)]
-HALVES = [(0, 512, 128), (512, T, 0)]
-LAST = [(0, 256, 256), (256, 576, 0), (576, 832, 0), (832, T, 0)]
-CHUNKS = [WHOLE] * 2 + [HALVES] * 4 + [[(0, 512, 0), (512, T, 0)], LAST]
+HALVES = [(0, 512, 0), (512, T, 0)]
+LAST = [(0, 320, 320), (320, 576, 0), (576, 832, 0), (832, T, 0)]
+CHUNKS = [WHOLE] * 2 + [HALVES, [(0, 512, 0), (512, T, 224)]] * 2 + [HALVES, LAST]
 EARLY = [(0, 256), (256, 512)]
 QUARTERS = [(0, 128), (128, 256), (256, 384), (384, 512)]
 GROUPS = [(0, 256), (256, 384), (384, 512)]

@@ -18,10 +18,9 @@ PACK = 4
 K_PASS = P * PACK
 PASSES = K // K_PASS
 PAIRS = 2 * PASSES
-WHOLE = [(0, T, 608)]
 HALVES = [(0, 512, 0), (512, T, 0)]
-LAST = [(0, 320, 320), (320, 576, 0), (576, 832, 0), (832, T, 0)]
-CHUNKS = [WHOLE] * 2 + [HALVES, [(0, 512, 0), (512, T, 224)]] * 2 + [HALVES, LAST]
+LAST = [(0, 448, 0), (448, 832, 0), (832, T, 0)]
+CHUNKS = [[(0, T, 0)], [(0, T, 192)]] * 2 + [[(0, T, 0)], [(0, T, 448)], HALVES, LAST]
 EARLY = [(0, 256), (256, 512)]
 QUARTERS = [(0, 128), (128, 256), (256, 384), (384, 512)]
 GROUPS = [(0, 256), (256, 384), (384, 512)]

@@ -15,6 +15,7 @@ FP8X4 = mybir.dt.float8_e4m3fn_x4
 
 P = 128
 PACK = 4
+LINE = 4
 K_PASS = P * PACK
 PASSES = K // K_PASS
 PAIRS = 2 * PASSES
@@ -62,15 +63,20 @@ def tile_picked_pool_lin_bias_sub_e_kernel(tc, xT, w_words, w_scales, b, offs, o
         planes = [keep.tile([P, S], U8, name="plane_%d" % a, align_bytes=64) for a in range(PASSES)]
         accs = [psum.tile([P, j1 - j0], F32, name="acc_%d" % j0) for j0, j1 in GROUPS]
 
+        def round_tokens(copy, dst, src):
+            copy(
+                dst.rearrange("p (c i) j -> p c j i", i=LINE),
+                src.rearrange("p j (c i) -> p c j i", i=LINE),
+            )
+
         def round_pair(i):
             pairs = keep.tile([P, T, 2], BF16, name="pairs_%d" % i)
             for c, (t0, t1, share) in enumerate(CHUNKS[i]):
-                src = raw[i, c][:].rearrange("p j t -> p t j")
                 cut = t1 - t0 - share
                 if cut > 0:
-                    nc.scalar.copy(pairs[:, t0 : t0 + cut, :], src[:, :cut, :])
+                    round_tokens(nc.scalar.copy, pairs[:, t0 : t0 + cut, :], raw[i, c][:, :, :cut])
                 if share > 0:
-                    nc.vector.tensor_copy(pairs[:, t0 + cut : t1, :], src[:, cut:, :])
+                    round_tokens(nc.vector.tensor_copy, pairs[:, t0 + cut : t1, :], raw[i, c][:, :, cut:])
             return pairs[:].rearrange("p t j -> p (t j)").bitcast(U32)
 
         def gather(i, window, j0, j1):
@@ -82,8 +88,8 @@ def tile_picked_pool_lin_bias_sub_e_kernel(tc, xT, w_words, w_scales, b, offs, o
 
         def weave(copy, a, j0, j1):
             copy(
-                grouped[a][:, PACK * j0 : PACK * j1].bitcast(F32).rearrange("p (n u) -> p n u", u=2),
-                picked[a][:, :, 2 * j0 : 2 * j1].bitcast(F32).rearrange("p u n -> p n u"),
+                grouped[a][:, PACK * j0 : PACK * j1].bitcast(F32).rearrange("p (c i u) -> p c u i", i=LINE, u=2),
+                picked[a][:, :, 2 * j0 : 2 * j1].bitcast(F32).rearrange("p u (c i) -> p c u i", i=LINE),
             )
 
         def quantise(a, j0, j1):

@@ -20,8 +20,8 @@ K_PASS = P * PACK
 PASSES = K // K_PASS
 PAIRS = 2 * PASSES
 HALVES = [(0, 512, 0), (512, T, 0)]
-LAST = [(0, 448, 0), (448, 832, 0), (832, T, 0)]
-CHUNKS = [[(0, T, 0)], [(0, T, 192)]] * 2 + [[(0, T, 0)], [(0, T, 448)], HALVES, LAST]
+LAST = [(0, 448, 0), (448, 832, 224), (832, T, 0)]
+CHUNKS = [[(0, T, 0)], [(0, T, 384)]] * 3 + [HALVES, LAST]
 EARLY = [(0, 256), (256, 512)]
 QUARTERS = [(0, 128), (128, 256), (256, 384), (384, 512)]
 GROUPS = [(0, 256), (256, 384), (384, 512)]
@@ -76,7 +76,7 @@ def tile_picked_pool_lin_bias_sub_e_kernel(tc, xT, w_words, w_scales, b, offs, o
                 if cut > 0:
                     round_tokens(nc.scalar.copy, pairs[:, t0 : t0 + cut, :], raw[i, c][:, :, :cut])
                 if share > 0:
-                    round_tokens(nc.vector.tensor_copy, pairs[:, t0 + cut : t1, :], raw[i, c][:, :, cut:])
+                    nc.gpsimd.tensor_copy(pairs[:, t0 + cut : t1, :], raw[i, c][:, :, cut:].rearrange("p j t -> p t j"))
             return pairs[:].rearrange("p t j -> p (t j)").bitcast(U32)
 
         def gather(i, window, j0, j1):

@@ -19,9 +19,9 @@ LINE = 4
 K_PASS = P * PACK
 PASSES = K // K_PASS
 PAIRS = 2 * PASSES
-HALVES = [(0, 512, 0), (512, T, 0)]
-LAST = [(0, 448, 0), (448, 832, 224), (832, T, 0)]
-CHUNKS = [[(0, T, 0)], [(0, T, 384)]] * 3 + [HALVES, LAST]
+SECOND_LAST = [(0, 640, 256), (640, T, 0)]
+LAST = [(0, 448, 0), (448, 832, 192), (832, T, 0)]
+CHUNKS = [[(0, T, 128)], [(0, T, 320)]] * 3 + [SECOND_LAST, LAST]
 EARLY = [(0, 256), (256, 512)]
 QUARTERS = [(0, 128), (128, 256), (256, 384), (384, 512)]
 GROUPS = [(0, 256), (256, 384), (384, 512)]
@@ -34,7 +34,7 @@ def tile_picked_pool_lin_bias_sub_e_kernel(tc, xT, w_words, w_scales, b, offs, o
         psum = ctx.enter_context(tc.psum_pool(name="psum", bufs=1))
 
         offsets = keep.tile([P, S // 16], U16, name="offsets")
-        w_codes = keep.tile([P, PASSES, N], U32, name="w_codes", align_bytes=64)
+        w_codes = [keep.tile([P, N], U32, name="w_codes_%d" % a, align_bytes=64) for a in range(PASSES)]
         w_plane = keep.tile([P, N], U8, name="w_plane", align_bytes=64)
         bias = keep.tile([P, 1], F32, name="bias")
         nc.vector.memset(w_plane[:].bitcast(I32), 0)
@@ -52,7 +52,8 @@ def tile_picked_pool_lin_bias_sub_e_kernel(tc, xT, w_words, w_scales, b, offs, o
                 nc.sync.dma_start(raw[i, c][:], x_rows[a, :, 2 * u : 2 * u + 2, t0:t1])
                 if (i, c) == (0, 0):
                     nc.sync.dma_start(offsets[:], offs)
-        nc.sync.dma_start(w_codes[:].bitcast(I32), w_words.rearrange("a p m r -> p a (m r)").bitcast(I32))
+        for a in range(PASSES):
+            nc.sync.dma_start(w_codes[a][:].bitcast(I32), w_words[a].rearrange("p m r -> p (m r)").bitcast(I32))
         nc.sync.dma_start(bias[:], b)
 
         pooled = keep.tile([P, V], F32, name="pooled")
@@ -103,7 +104,7 @@ def tile_picked_pool_lin_bias_sub_e_kernel(tc, xT, w_words, w_scales, b, offs, o
             j0, j1 = GROUPS[g]
             nc.tensor.matmul_mx(
                 out=accs[g][:],
-                lhsT=w_codes[:, a, :].bitcast(FP8X4),
+                lhsT=w_codes[a][:].bitcast(FP8X4),
                 lhsT_scale=w_plane[4 * a :, :],
                 rhs=codes[a][:, j0:j1].bitcast(FP8X4),
                 rhs_scale=planes[a][:, j0:j1],
@@ -125,8 +126,8 @@ def tile_picked_pool_lin_bias_sub_e_kernel(tc, xT, w_words, w_scales, b, offs, o
             window = round_pair(2 * a + 3)
         for j0, j1 in QUARTERS:
             gather(2 * last + 1, window, j0, j1)
-        for g in range(len(GROUPS)):
-            for a in range(last):
+        for a in range(last):
+            for g in range(len(GROUPS)):
                 multiply(a, g)
         for j0, j1 in QUARTERS:
             weave(nc.scalar.copy, last, j0, j1)
@@ -140,5 +141,7 @@ def tile_picked_pool_lin_bias_sub_e_kernel(tc, xT, w_words, w_scales, b, offs, o
                 mybir.AxisListType.X,
                 mybir.AluOpType.max,
             )
-        nc.vector.tensor_scalar_add(result[:], pooled[:], bias[:])
-        nc.sync.dma_start(out, result[:])
+        for j0, j1 in GROUPS:
+            centres = slice(j0 // D, j1 // D)
+            nc.vector.tensor_scalar_add(result[:, centres], pooled[:, centres], bias[:])
+            nc.sync.dma_start(out[:, centres], result[:, centres])

@@ -19,12 +19,13 @@ LINE = 4
 K_PASS = P * PACK
 PASSES = K // K_PASS
 PAIRS = 2 * PASSES
-SECOND_LAST = [(0, 640, 256), (640, T, 0)]
-LAST = [(0, 448, 0), (448, 832, 192), (832, T, 0)]
+SECOND_LAST = [(0, 640, 320), (640, T, 0)]
+LAST = [(0, 448, 0), (448, 832, 224), (832, T, 0)]
 CHUNKS = [[(0, T, 128)], [(0, T, 320)]] * 3 + [SECOND_LAST, LAST]
 EARLY = [(0, 256), (256, 512)]
 QUARTERS = [(0, 128), (128, 256), (256, 384), (384, 512)]
-GROUPS = [(0, 256), (256, 384), (384, 512)]
+GROUPS = QUARTERS
+STORES = [(0, 64), (64, 96), (96, 128)]
 
 
 def tile_picked_pool_lin_bias_sub_e_kernel(tc, xT, w_words, w_scales, b, offs, out):
@@ -141,7 +142,11 @@ def tile_picked_pool_lin_bias_sub_e_kernel(tc, xT, w_words, w_scales, b, offs, o
                 mybir.AxisListType.X,
                 mybir.AluOpType.max,
             )
-        for j0, j1 in GROUPS:
-            centres = slice(j0 // D, j1 // D)
-            nc.vector.tensor_scalar_add(result[:, centres], pooled[:, centres], bias[:])
-            nc.sync.dma_start(out[:, centres], result[:, centres])
+        for v0, v1 in STORES:
+            if v1 < V:
+                nc.scalar.activation(
+                    result[:, v0:v1], pooled[:, v0:v1], mybir.ActivationFunctionType.Identity, bias=bias[:]
+                )
+            else:
+                nc.vector.tensor_scalar_add(result[:, v0:v1], pooled[:, v0:v1], bias[:])
+            nc.sync.dma_start(out[:, v0:v1], result[:, v0:v1])

@@ -20,8 +20,8 @@ K_PASS = P * PACK
 PASSES = K // K_PASS
 PAIRS = 2 * PASSES
 SECOND_LAST = [(0, 640, 320), (640, T, 0)]
-LAST = [(0, 448, 0), (448, 832, 224), (832, T, 0)]
-CHUNKS = [[(0, T, 128)], [(0, T, 320)]] * 3 + [SECOND_LAST, LAST]
+LAST = [(0, 448, 0), (448, 832, 256), (832, T, 0)]
+CHUNKS = [[(0, T, 128)], [(0, T, 384)]] * 3 + [SECOND_LAST, LAST]
 EARLY = [(0, 256), (256, 512)]
 QUARTERS = [(0, 128), (128, 256), (256, 384), (384, 512)]
 GROUPS = QUARTERS
@@ -78,7 +78,7 @@ def tile_picked_pool_lin_bias_sub_e_kernel(tc, xT, w_words, w_scales, b, offs, o
                 if cut > 0:
                     round_tokens(nc.scalar.copy, pairs[:, t0 : t0 + cut, :], raw[i, c][:, :, :cut])
                 if share > 0:
-                    nc.gpsimd.tensor_copy(pairs[:, t0 + cut : t1, :], raw[i, c][:, :, cut:].rearrange("p j t -> p t j"))
+                    nc.gpsimd.tensor_copy(pairs[:, t0 + cut : t1, :].rearrange("p t j -> p j t"), raw[i, c][:, :, cut:])
             return pairs[:].rearrange("p t j -> p (t j)").bitcast(U32)
 
         def gather(i, window, j0, j1):

@@ -41,8 +41,6 @@ def tile_picked_pool_lin_bias_sub_e_kernel(tc, xT, w_words, w_scales, b, offs, o
         nc.vector.memset(w_plane[:].bitcast(I32), 0)
 
         scale_words = w_scales.bitcast(I32)
-        for q in range(4):
-            nc.scalar.dma_start(w_plane[32 * q : 32 * q + 16, :].bitcast(I32), scale_words[:, 4 * q : 4 * q + 4, :])
 
         x_rows = xT.rearrange("(a p j) t -> a p j t", p=P, j=PACK)
         raw = {}
@@ -53,6 +51,11 @@ def tile_picked_pool_lin_bias_sub_e_kernel(tc, xT, w_words, w_scales, b, offs, o
                 nc.sync.dma_start(raw[i, c][:], x_rows[a, :, 2 * u : 2 * u + 2, t0:t1])
                 if (i, c) == (0, 0):
                     nc.sync.dma_start(offsets[:], offs)
+                if (i, c) == (PAIRS - 1, 0):
+                    for q in range(4):
+                        nc.sync.dma_start(
+                            w_plane[32 * q : 32 * q + 16, :].bitcast(I32), scale_words[:, 4 * q : 4 * q + 4, :]
+                        )
         for a in range(PASSES):
             nc.sync.dma_start(w_codes[a][:].bitcast(I32), w_words[a].rearrange("p m r -> p (m r)").bitcast(I32))
         nc.sync.dma_start(bias[:], b)

@@ -21,7 +21,7 @@ PASSES = K // K_PASS
 PAIRS = 2 * PASSES
 SECOND_LAST = [(0, 640, 320), (640, T, 0)]
 LAST = [(0, 448, 0), (448, 832, 256), (832, T, 0)]
-CHUNKS = [[(0, T, 128)], [(0, T, 384)]] * 3 + [SECOND_LAST, LAST]
+CHUNKS = [[(0, T, 128)], [(0, T, 448)]] * 3 + [SECOND_LAST, LAST]
 EARLY = [(0, 256), (256, 512)]
 QUARTERS = [(0, 128), (128, 256), (256, 384), (384, 512)]
 GROUPS = QUARTERS
@@ -81,7 +81,7 @@ def tile_picked_pool_lin_bias_sub_e_kernel(tc, xT, w_words, w_scales, b, offs, o
                 if cut > 0:
                     round_tokens(nc.scalar.copy, pairs[:, t0 : t0 + cut, :], raw[i, c][:, :, :cut])
                 if share > 0:
-                    nc.gpsimd.tensor_copy(pairs[:, t0 + cut : t1, :].rearrange("p t j -> p j t"), raw[i, c][:, :, cut:])
+                    round_tokens(nc.gpsimd.tensor_copy, pairs[:, t0 + cut : t1, :], raw[i, c][:, :, cut:])
             return pairs[:].rearrange("p t j -> p (t j)").bitcast(U32)
 
         def gather(i, window, j0, j1):

@@ -12,19 +12,18 @@ U32 = mybir.dt.uint32
 U16 = mybir.dt.uint16
 U8 = mybir.dt.uint8
 FP8X4 = mybir.dt.float8_e4m3fn_x4
+COPY = mybir.ActivationFunctionType.Copy
+IDENTITY = mybir.ActivationFunctionType.Identity
 
 P = 128
 PACK = 4
-LINE = 4
+LINE = 2
 K_PASS = P * PACK
 PASSES = K // K_PASS
-PAIRS = 2 * PASSES
-SECOND_LAST = [(0, 640, 320), (640, T, 0)]
-LAST = [(0, 448, 0), (448, 832, 256), (832, T, 0)]
-CHUNKS = [[(0, T, 128)], [(0, T, 448)]] * 3 + [SECOND_LAST, LAST]
-EARLY = [(0, 256), (256, 512)]
+LOADS = [[(0, 2), (2, 2)], [(0, 2), (2, 2)], [(0, 2), (2, 1), (3, 1)], [(0, 2), (2, 1), (3, 1)]]
+CUT = 128
+HALF = S // 2
 QUARTERS = [(0, 128), (128, 256), (256, 384), (384, 512)]
-GROUPS = QUARTERS
 STORES = [(0, 64), (64, 96), (96, 128)]
 
 
@@ -41,17 +40,19 @@ def tile_picked_pool_lin_bias_sub_e_kernel(tc, xT, w_words, w_scales, b, offs, o
         nc.vector.memset(w_plane[:].bitcast(I32), 0)
 
         scale_words = w_scales.bitcast(I32)
+        last = PASSES - 1
 
-        x_rows = xT.rearrange("(a p j) t -> a p j t", p=P, j=PACK)
-        raw = {}
-        for i in range(PAIRS):
-            a, u = divmod(i, 2)
-            for c, (t0, t1, share) in enumerate(CHUNKS[i]):
-                raw[i, c] = keep.tile([P, 2, t1 - t0], F32, name="raw_%d_%d" % (i, c))
-                nc.sync.dma_start(raw[i, c][:], x_rows[a, :, 2 * u : 2 * u + 2, t0:t1])
-                if (i, c) == (0, 0):
+        x_rows = xT.rearrange("(a p t) n -> a p t n", p=P, t=PACK)
+        window = {}
+        for a in range(PASSES):
+            for t0, count in LOADS[a]:
+                raw = keep.tile([P, count, T], F32, name="raw_%d_%d" % (a, t0))
+                nc.sync.dma_start(raw[:], x_rows[a, :, t0 : t0 + count, :])
+                for t in range(count):
+                    window[a, t0 + t] = raw[:, t, :]
+                if (a, t0) == (0, 0):
                     nc.sync.dma_start(offsets[:], offs)
-                if (i, c) == (PAIRS - 1, 0):
+                if (a, t0) == (last, 2):
                     for q in range(4):
                         nc.sync.dma_start(
                             w_plane[32 * q : 32 * q + 16, :].bitcast(I32), scale_words[:, 4 * q : 4 * q + 4, :]
@@ -62,39 +63,22 @@ def tile_picked_pool_lin_bias_sub_e_kernel(tc, xT, w_words, w_scales, b, offs, o
 
         pooled = keep.tile([P, V], F32, name="pooled")
         result = keep.tile([P, V], F32, name="result")
-        picked = [keep.tile([P, 2, 2 * S], BF16, name="picked_%d" % a) for a in range(PASSES)]
+        picked = [keep.tile([P, PACK, S], F32, name="picked_%d" % a) for a in range(PASSES)]
         grouped = [keep.tile([P, PACK * S], BF16, name="grouped_%d" % a, align_bytes=64) for a in range(PASSES)]
         codes = [keep.tile([P, S], U32, name="codes_%d" % a, align_bytes=64) for a in range(PASSES)]
         planes = [keep.tile([P, S], U8, name="plane_%d" % a, align_bytes=64) for a in range(PASSES)]
-        accs = [psum.tile([P, j1 - j0], F32, name="acc_%d" % j0) for j0, j1 in GROUPS]
+        accs = [psum.tile([P, j1 - j0], F32, name="acc_%d" % j0) for j0, j1 in QUARTERS]
 
-        def round_tokens(copy, dst, src):
-            copy(
-                dst.rearrange("p (c i) j -> p c j i", i=LINE),
-                src.rearrange("p j (c i) -> p c j i", i=LINE),
-            )
+        def gather_v(a, t, j0, j1):
+            nc.vector.tensor_copy(picked[a][:, t, j0:j1], window[a, t].indirect(offsets[:, j0 // 16 : j1 // 16]))
 
-        def round_pair(i):
-            pairs = keep.tile([P, T, 2], BF16, name="pairs_%d" % i)
-            for c, (t0, t1, share) in enumerate(CHUNKS[i]):
-                cut = t1 - t0 - share
-                if cut > 0:
-                    round_tokens(nc.scalar.copy, pairs[:, t0 : t0 + cut, :], raw[i, c][:, :, :cut])
-                if share > 0:
-                    round_tokens(nc.gpsimd.tensor_copy, pairs[:, t0 + cut : t1, :], raw[i, c][:, :, cut:])
-            return pairs[:].rearrange("p t j -> p (t j)").bitcast(U32)
-
-        def gather(i, window, j0, j1):
-            a, u = divmod(i, 2)
-            nc.vector.tensor_copy(
-                picked[a][:, u, 2 * j0 : 2 * j1].bitcast(U32),
-                window.indirect(offsets[:, j0 // 16 : j1 // 16]),
-            )
+        def gather_s(a, t, j0, j1):
+            nc.scalar.activation(picked[a][:, t, j0:j1], window[a, t].indirect(offsets[:, j0 // 16 : j1 // 16]), COPY)
 
         def weave(copy, a, j0, j1):
             copy(
-                grouped[a][:, PACK * j0 : PACK * j1].bitcast(F32).rearrange("p (c i u) -> p c u i", i=LINE, u=2),
-                picked[a][:, :, 2 * j0 : 2 * j1].bitcast(F32).rearrange("p u (c i) -> p c u i", i=LINE),
+                grouped[a][:, PACK * j0 : PACK * j1].rearrange("p (c i t) -> p c t i", i=LINE, t=PACK),
+                picked[a][:, :, j0:j1].rearrange("p t (c i) -> p c t i", i=LINE),
             )
 
         def quantise(a, j0, j1):
@@ -105,7 +89,7 @@ def tile_picked_pool_lin_bias_sub_e_kernel(tc, xT, w_words, w_scales, b, offs, o
             )
 
         def multiply(a, g):
-            j0, j1 = GROUPS[g]
+            j0, j1 = QUARTERS[g]
             nc.tensor.matmul_mx(
                 out=accs[g][:],
                 lhsT=w_codes[a][:].bitcast(FP8X4),
@@ -113,32 +97,52 @@ def tile_picked_pool_lin_bias_sub_e_kernel(tc, xT, w_words, w_scales, b, offs, o
                 rhs=codes[a][:, j0:j1].bitcast(FP8X4),
                 rhs_scale=planes[a][:, j0:j1],
                 start=(a == 0),
-                stop=(a == PASSES - 1),
+                stop=(a == last),
             )
 
-        last = PASSES - 1
-        gather(0, round_pair(0), 0, S)
-        window = round_pair(1)
         for a in range(last):
-            for j0, j1 in EARLY:
-                gather(2 * a + 1, window, j0, j1)
-            for j0, j1 in EARLY:
-                weave(nc.vector.tensor_copy, a, j0, j1)
-            for j0, j1 in EARLY:
-                quantise(a, j0, j1)
-            gather(2 * a + 2, round_pair(2 * a + 2), 0, S)
-            window = round_pair(2 * a + 3)
-        for j0, j1 in QUARTERS:
-            gather(2 * last + 1, window, j0, j1)
+            if a == 0:
+                gather_s(a, 1, 0, HALF)
+                gather_v(a, 0, 0, S)
+            else:
+                gather_s(a, 0, 0, S)
+                gather_s(a, 1, 0, HALF)
+            gather_v(a, 1, HALF, S)
+            if a < last - 1:
+                gather_s(a, 2, 0, HALF)
+                gather_v(a, 3, 0, HALF)
+                gather_s(a, 2, HALF, S)
+                gather_v(a, 3, HALF, S)
+            else:
+                gather_v(a, 2, 0, CUT)
+                gather_s(a, 2, CUT, S)
+                gather_v(a, 3, 0, HALF)
+                gather_s(a, 3, HALF, S)
+            weave(nc.scalar.copy, a, 384, S)
+            weave(nc.vector.tensor_copy, a, 0, HALF)
+            weave(nc.vector.tensor_copy, a, HALF, 384)
+            quantise(a, 0, HALF)
+            quantise(a, HALF, S)
+        gather_s(last, 0, 0, S)
+        gather_v(last, 1, 0, S)
+        gather_v(last, 2, 0, 192)
+        gather_s(last, 2, 192, S)
+        gather_v(last, 3, *QUARTERS[0])
+        for g in (2, 1, 3):
+            gather_s(last, 3, *QUARTERS[g])
         for a in range(last):
-            for g in range(len(GROUPS)):
+            for g in range(len(QUARTERS)):
                 multiply(a, g)
-        for j0, j1 in QUARTERS:
-            weave(nc.scalar.copy, last, j0, j1)
-        for g, (j0, j1) in enumerate(GROUPS):
-            quantise(last, j0, j1)
+        weave(nc.scalar.copy, last, *QUARTERS[2])
+        weave(nc.vector.tensor_copy, last, *QUARTERS[0])
+        weave(nc.vector.tensor_copy, last, *QUARTERS[1])
+        quantise(last, *QUARTERS[0])
+        weave(nc.vector.tensor_copy, last, *QUARTERS[3])
+        for g in (1, 2, 3):
+            quantise(last, *QUARTERS[g])
+        for g in range(len(QUARTERS)):
             multiply(last, g)
-        for g, (j0, j1) in enumerate(GROUPS):
+        for g, (j0, j1) in enumerate(QUARTERS):
             nc.vector.tensor_reduce(
                 pooled[:, j0 // D : j1 // D],
                 accs[g][:].rearrange("p (v d) -> p v d", d=D),
@@ -147,9 +151,7 @@ def tile_picked_pool_lin_bias_sub_e_kernel(tc, xT, w_words, w_scales, b, offs, o
             )
         for v0, v1 in STORES:
             if v1 < V:
-                nc.scalar.activation(
-                    result[:, v0:v1], pooled[:, v0:v1], mybir.ActivationFunctionType.Identity, bias=bias[:]
-                )
+                nc.scalar.activation(result[:, v0:v1], pooled[:, v0:v1], IDENTITY, bias=bias[:])
             else:
                 nc.vector.tensor_scalar_add(result[:, v0:v1], pooled[:, v0:v1], bias[:])
             nc.sync.dma_start(out[:, v0:v1], result[:, v0:v1])

@@ -127,18 +127,19 @@ def tile_picked_pool_lin_bias_sub_e_kernel(tc, xT, w_words, w_scales, b, offs, o
         gather_v(last, 1, 0, S)
         gather_v(last, 2, 0, 192)
         gather_s(last, 2, 192, S)
-        gather_v(last, 3, *QUARTERS[0])
-        for g in (2, 1, 3):
-            gather_s(last, 3, *QUARTERS[g])
+        gather_v(last, 3, *QUARTERS[3])
+        gather_v(last, 3, *QUARTERS[2])
+        gather_s(last, 3, *QUARTERS[0])
+        gather_s(last, 3, *QUARTERS[1])
         for a in range(last):
             for g in range(len(QUARTERS)):
                 multiply(a, g)
         weave(nc.scalar.copy, last, *QUARTERS[2])
+        weave(nc.scalar.copy, last, 384, 448)
         weave(nc.vector.tensor_copy, last, *QUARTERS[0])
         weave(nc.vector.tensor_copy, last, *QUARTERS[1])
-        quantise(last, *QUARTERS[0])
-        weave(nc.vector.tensor_copy, last, *QUARTERS[3])
-        for g in (1, 2, 3):
+        weave(nc.vector.tensor_copy, last, 448, S)
+        for g in range(len(QUARTERS)):
             quantise(last, *QUARTERS[g])
         for g in range(len(QUARTERS)):
             multiply(last, g)

@@ -37,7 +37,7 @@ def tile_picked_pool_lin_bias_sub_e_kernel(tc, xT, w_words, w_scales, b, offs, o
         w_codes = [keep.tile([P, N], U32, name="w_codes_%d" % a, align_bytes=64) for a in range(PASSES)]
         w_plane = keep.tile([P, N], U8, name="w_plane", align_bytes=64)
         bias = keep.tile([P, 1], F32, name="bias")
-        nc.vector.memset(w_plane[:].bitcast(I32), 0)
+        nc.gpsimd.memset(w_plane[:].bitcast(I32), 0)
 
         scale_words = w_scales.bitcast(I32)
         last = PASSES - 1
@@ -52,7 +52,6 @@ def tile_picked_pool_lin_bias_sub_e_kernel(tc, xT, w_words, w_scales, b, offs, o
                     window[a, t0 + t] = raw[:, t, :]
                 if (a, t0) == (0, 0):
                     nc.sync.dma_start(offsets[:], offs)
-                if (a, t0) == (last, 2):
                     for q in range(4):
                         nc.sync.dma_start(
                             w_plane[32 * q : 32 * q + 16, :].bitcast(I32), scale_words[:, 4 * q : 4 * q + 4, :]

@@ -20,7 +20,7 @@ PACK = 4
 LINE = 2
 K_PASS = P * PACK
 PASSES = K // K_PASS
-LOADS = [[(0, 2), (2, 2)], [(0, 2), (2, 2)], [(0, 2), (2, 1), (3, 1)], [(0, 2), (2, 1), (3, 1)]]
+LOADS = [[(0, 2), (2, 2)], [(0, 2), (2, 2)], [(0, 2), (2, 1), (3, 1)], [(0, 1), (1, 1), (2, 1), (3, 1)]]
 CUT = 128
 HALF = S // 2
 QUARTERS = [(0, 128), (128, 256), (256, 384), (384, 512)]
@@ -43,6 +43,7 @@ def tile_picked_pool_lin_bias_sub_e_kernel(tc, xT, w_words, w_scales, b, offs, o
         last = PASSES - 1
 
         x_rows = xT.rearrange("(a p t) n -> a p t n", p=P, t=PACK)
+        w_rows = w_words.rearrange("a p m r -> a p (m r)").bitcast(I32)
         window = {}
         for a in range(PASSES):
             for t0, count in LOADS[a]:
@@ -50,14 +51,16 @@ def tile_picked_pool_lin_bias_sub_e_kernel(tc, xT, w_words, w_scales, b, offs, o
                 nc.sync.dma_start(raw[:], x_rows[a, :, t0 : t0 + count, :])
                 for t in range(count):
                     window[a, t0 + t] = raw[:, t, :]
+                if (a, t0) == (last, 2):
+                    nc.sync.dma_start(w_codes[0][:].bitcast(I32), w_rows[0])
                 if (a, t0) == (0, 0):
                     nc.sync.dma_start(offsets[:], offs)
                     for q in range(4):
                         nc.sync.dma_start(
                             w_plane[32 * q : 32 * q + 16, :].bitcast(I32), scale_words[:, 4 * q : 4 * q + 4, :]
                         )
-        for a in range(PASSES):
-            nc.sync.dma_start(w_codes[a][:].bitcast(I32), w_words[a].rearrange("p m r -> p (m r)").bitcast(I32))
+        for a in range(1, PASSES):
+            nc.sync.dma_start(w_codes[a][:].bitcast(I32), w_rows[a])
         nc.sync.dma_start(bias[:], b)
 
         pooled = keep.tile([P, V], F32, name="pooled")
@@ -123,7 +126,8 @@ def tile_picked_pool_lin_bias_sub_e_kernel(tc, xT, w_words, w_scales, b, offs, o
             quantise(a, 0, HALF)
             quantise(a, HALF, S)
         gather_s(last, 0, 0, S)
-        gather_v(last, 1, 0, S)
+        gather_v(last, 1, 0, 320)
+        gather_s(last, 1, 320, S)
         gather_v(last, 2, 0, 192)
         gather_s(last, 2, 192, S)
         gather_v(last, 3, *QUARTERS[3])

@@ -17,7 +17,7 @@ IDENTITY = mybir.ActivationFunctionType.Identity
 
 P = 128
 PACK = 4
-LINE = 2
+LINE = 4
 K_PASS = P * PACK
 PASSES = K // K_PASS
 LOADS = [[(0, 2), (2, 2)], [(0, 2), (2, 2)], [(0, 2), (2, 1), (3, 1)], [(0, 1), (1, 1), (2, 1), (3, 1)]]

@@ -17,11 +17,11 @@ IDENTITY = mybir.ActivationFunctionType.Identity
 
 P = 128
 PACK = 4
-LINE = 4
+LINE = 2
 K_PASS = P * PACK
 PASSES = K // K_PASS
 LOADS = [[(0, 2), (2, 2)], [(0, 2), (2, 2)], [(0, 2), (2, 1), (3, 1)], [(0, 1), (1, 1), (2, 1), (3, 1)]]
-CUT = 128
+CUT = 320
 HALF = S // 2
 QUARTERS = [(0, 128), (128, 256), (256, 384), (384, 512)]
 STORES = [(0, 64), (64, 96), (96, 128)]
@@ -128,8 +128,8 @@ def tile_picked_pool_lin_bias_sub_e_kernel(tc, xT, w_words, w_scales, b, offs, o
         gather_s(last, 0, 0, S)
         gather_v(last, 1, 0, 320)
         gather_s(last, 1, 320, S)
-        gather_v(last, 2, 0, 192)
-        gather_s(last, 2, 192, S)
+        gather_v(last, 2, 0, HALF)
+        gather_s(last, 2, HALF, S)
         gather_v(last, 3, *QUARTERS[3])
         gather_v(last, 3, *QUARTERS[2])
         gather_s(last, 3, *QUARTERS[0])

@@ -20,11 +20,12 @@ PACK = 4
 LINE = 2
 K_PASS = P * PACK
 PASSES = K // K_PASS
-LOADS = [[(0, 2), (2, 2)], [(0, 2), (2, 2)], [(0, 2), (2, 1), (3, 1)], [(0, 1), (1, 1), (2, 1), (3, 1)]]
+LOADS = [[(0, 2), (2, 2)], [(0, 2), (2, 1), (3, 1)], [(0, 2), (2, 1), (3, 1)], [(0, 1), (1, 1), (2, 1), (3, 1)]]
+FIRST_S = [256, 256, 128]
 CUT = 320
 HALF = S // 2
 QUARTERS = [(0, 128), (128, 256), (256, 384), (384, 512)]
-STORES = [(0, 64), (64, 96), (96, 128)]
+STORES = [(0, 96), (96, 128)]
 
 
 def tile_picked_pool_lin_bias_sub_e_kernel(tc, xT, w_words, w_scales, b, offs, out):
@@ -104,13 +105,13 @@ def tile_picked_pool_lin_bias_sub_e_kernel(tc, xT, w_words, w_scales, b, offs, o
 
         for a in range(last):
             if a == 0:
-                gather_s(a, 1, 0, HALF)
+                gather_s(a, 1, 0, FIRST_S[a])
                 gather_v(a, 0, 0, S)
             else:
                 gather_s(a, 0, 0, S)
-                gather_s(a, 1, 0, HALF)
-            gather_v(a, 1, HALF, S)
-            if a < last - 1:
+                gather_s(a, 1, 0, FIRST_S[a])
+            gather_v(a, 1, FIRST_S[a], S)
+            if a == 0:
                 gather_s(a, 2, 0, HALF)
                 gather_v(a, 3, 0, HALF)
                 gather_s(a, 2, HALF, S)

@@ -18,6 +18,7 @@ IDENTITY = mybir.ActivationFunctionType.Identity
 P = 128
 PACK = 4
 LINE = 2
+BURST = 256
 K_PASS = P * PACK
 PASSES = K // K_PASS
 LOADS = [[(0, 2), (2, 2)], [(0, 2), (2, 1), (3, 1)], [(0, 2), (2, 1), (3, 1)], [(0, 1), (1, 1), (2, 1), (3, 1)]]
@@ -35,7 +36,7 @@ def tile_picked_pool_lin_bias_sub_e_kernel(tc, xT, w_words, w_scales, b, offs, o
         psum = ctx.enter_context(tc.psum_pool(name="psum", bufs=1))
 
         offsets = keep.tile([P, S // 16], U16, name="offsets")
-        w_codes = [keep.tile([P, N], U32, name="w_codes_%d" % a, align_bytes=64) for a in range(PASSES)]
+        w_codes = [keep.tile([P, N], U32, name="w_codes_%d" % a, align_bytes=BURST) for a in range(PASSES)]
         w_plane = keep.tile([P, N], U8, name="w_plane", align_bytes=64)
         bias = keep.tile([P, 1], F32, name="bias")
         nc.gpsimd.memset(w_plane[:].bitcast(I32), 0)
@@ -48,7 +49,7 @@ def tile_picked_pool_lin_bias_sub_e_kernel(tc, xT, w_words, w_scales, b, offs, o
         window = {}
         for a in range(PASSES):
             for t0, count in LOADS[a]:
-                raw = keep.tile([P, count, T], F32, name="raw_%d_%d" % (a, t0))
+                raw = keep.tile([P, count, T], F32, name="raw_%d_%d" % (a, t0), align_bytes=BURST)
                 nc.sync.dma_start(raw[:], x_rows[a, :, t0 : t0 + count, :])
                 for t in range(count):
                     window[a, t0 + t] = raw[:, t, :]
@@ -65,7 +66,7 @@ def tile_picked_pool_lin_bias_sub_e_kernel(tc, xT, w_words, w_scales, b, offs, o
         nc.sync.dma_start(bias[:], b)
 
         pooled = keep.tile([P, V], F32, name="pooled")
-        result = keep.tile([P, V], F32, name="result")
+        result = keep.tile([P, V], F32, name="result", align_bytes=BURST)
         picked = [keep.tile([P, PACK, S], F32, name="picked_%d" % a) for a in range(PASSES)]
         grouped = [keep.tile([P, PACK * S], BF16, name="grouped_%d" % a, align_bytes=64) for a in range(PASSES)]
         codes = [keep.tile([P, S], U32, name="codes_%d" % a, align_bytes=64) for a in range(PASSES)]

@@ -21,9 +21,9 @@ LINE = 2
 BURST = 256
 K_PASS = P * PACK
 PASSES = K // K_PASS
-LOADS = [[(0, 2), (2, 2)], [(0, 2), (2, 1), (3, 1)], [(0, 2), (2, 1), (3, 1)], [(0, 1), (1, 1), (2, 1), (3, 1)]]
-FIRST_S = [256, 256, 128]
-CUT = 320
+LOADS = [[(0, 2), (2, 2)], [(0, 2), (2, 2)], [(0, 2), (2, 1), (3, 1)], [(0, 2), (2, 1), (3, 1)]]
+FIRST_S = [256, 256, 192, 160]
+CUT = 224
 HALF = S // 2
 QUARTERS = [(0, 128), (128, 256), (256, 384), (384, 512)]
 STORES = [(0, 96), (96, 128)]
@@ -104,7 +104,7 @@ def tile_picked_pool_lin_bias_sub_e_kernel(tc, xT, w_words, w_scales, b, offs, o
                 stop=(a == last),
             )
 
-        for a in range(last):
+        for a in range(PASSES):
             if a == 0:
                 gather_s(a, 1, 0, FIRST_S[a])
                 gather_v(a, 0, 0, S)
@@ -113,23 +113,27 @@ def tile_picked_pool_lin_bias_sub_e_kernel(tc, xT, w_words, w_scales, b, offs, o
                 gather_s(a, 1, 0, FIRST_S[a])
             gather_v(a, 1, FIRST_S[a], S)
             if a == 0:
-                gather_s(a, 2, 0, HALF)
-                gather_v(a, 3, 0, HALF)
-                gather_s(a, 2, HALF, S)
-                gather_v(a, 3, HALF, S)
-            else:
-                gather_v(a, 2, 0, CUT)
-                gather_s(a, 2, CUT, S)
-                gather_v(a, 3, 0, HALF)
-                gather_s(a, 3, HALF, S)
-            weave(nc.scalar.copy, a, 384, S)
-            weave(nc.vector.tensor_copy, a, 0, HALF)
-            weave(nc.vector.tensor_copy, a, HALF, 384)
-            quantise(a, 0, HALF)
-            quantise(a, HALF, S)
-        gather_s(last, 0, 0, S)
-        gather_v(last, 1, 0, 320)
-        gather_s(last, 1, 320, S)
+                gather_s(a, 2, 0, S)
+                gather_v(a, 3, 0, S)
+                weave(nc.scalar.copy, a, 384, S)
+                weave(nc.vector.tensor_copy, a, 0, 384)
+                quantise(a, 0, S)
+            elif a < last:
+                if a == 1:
+                    gather_s(a, 2, 0, HALF)
+                    gather_v(a, 3, 0, HALF)
+                    gather_s(a, 2, HALF, S)
+                    gather_v(a, 3, HALF, S)
+                else:
+                    gather_v(a, 2, 0, CUT)
+                    gather_s(a, 2, CUT, S)
+                    gather_v(a, 3, 0, HALF)
+                    gather_s(a, 3, HALF, S)
+                weave(nc.scalar.copy, a, 384, S)
+                weave(nc.vector.tensor_copy, a, 0, HALF)
+                weave(nc.vector.tensor_copy, a, HALF, 384)
+                quantise(a, 0, HALF)
+                quantise(a, HALF, S)
         gather_v(last, 2, 0, HALF)
         gather_s(last, 2, HALF, S)
         gather_v(last, 3, *QUARTERS[3])

@@ -112,14 +112,8 @@ def tile_picked_pool_lin_bias_sub_e_kernel(tc, xT, w_words, w_scales, b, offs, o
                 gather_s(a, 0, 0, S)
                 gather_s(a, 1, 0, FIRST_S[a])
             gather_v(a, 1, FIRST_S[a], S)
-            if a == 0:
-                gather_s(a, 2, 0, S)
-                gather_v(a, 3, 0, S)
-                weave(nc.scalar.copy, a, 384, S)
-                weave(nc.vector.tensor_copy, a, 0, 384)
-                quantise(a, 0, S)
-            elif a < last:
-                if a == 1:
+            if a < last:
+                if a < last - 1:
                     gather_s(a, 2, 0, HALF)
                     gather_v(a, 3, 0, HALF)
                     gather_s(a, 2, HALF, S)

@@ -22,6 +22,7 @@ BURST = 256
 K_PASS = P * PACK
 PASSES = K // K_PASS
 LOADS = [[(0, 2), (2, 2)], [(0, 2), (2, 2)], [(0, 2), (2, 1), (3, 1)], [(0, 2), (2, 1), (3, 1)]]
+W_PIECES = [[(0, P)], [(0, P)], [(0, P // 2), (P // 2, P)], [(0, P // 2), (P // 2, P)]]
 FIRST_S = [256, 256, 192, 160]
 CUT = 224
 HALF = S // 2
@@ -53,16 +54,15 @@ def tile_picked_pool_lin_bias_sub_e_kernel(tc, xT, w_words, w_scales, b, offs, o
                 nc.sync.dma_start(raw[:], x_rows[a, :, t0 : t0 + count, :])
                 for t in range(count):
                     window[a, t0 + t] = raw[:, t, :]
-                if (a, t0) == (last, 2):
-                    nc.sync.dma_start(w_codes[0][:].bitcast(I32), w_rows[0])
                 if (a, t0) == (0, 0):
                     nc.sync.dma_start(offsets[:], offs)
                     for q in range(4):
                         nc.sync.dma_start(
                             w_plane[32 * q : 32 * q + 16, :].bitcast(I32), scale_words[:, 4 * q : 4 * q + 4, :]
                         )
-        for a in range(1, PASSES):
-            nc.sync.dma_start(w_codes[a][:].bitcast(I32), w_rows[a])
+        for a in range(PASSES):
+            for p0, p1 in W_PIECES[a]:
+                nc.sync.dma_start(w_codes[a][p0:p1, :].bitcast(I32), w_rows[a, p0:p1, :])
         nc.sync.dma_start(bias[:], b)
 
         pooled = keep.tile([P, V], F32, name="pooled")

@@ -27,7 +27,7 @@ FIRST_S = [256, 256, 192, 160]
 CUT = 224
 HALF = S // 2
 QUARTERS = [(0, 128), (128, 256), (256, 384), (384, 512)]
-STORES = [(0, 96), (96, 128)]
+STORES = [(0, 64), (64, 128)]
 
 
 def tile_picked_pool_lin_bias_sub_e_kernel(tc, xT, w_words, w_scales, b, offs, out):

from contextlib import ExitStack

import concourse.mybir as mybir

K, T, D, S, V, N = 2048, 1024, 4, 512, 128, 128
FLOPS = 2 * K * N * S

F32 = mybir.dt.float32
BF16 = mybir.dt.bfloat16
I32 = mybir.dt.int32
U32 = mybir.dt.uint32
U16 = mybir.dt.uint16
U8 = mybir.dt.uint8
FP8X4 = mybir.dt.float8_e4m3fn_x4
COPY = mybir.ActivationFunctionType.Copy
IDENTITY = mybir.ActivationFunctionType.Identity

P = 128
PACK = 4
LINE = 2
BURST = 256
K_PASS = P * PACK
PASSES = K // K_PASS
LOADS = [[(0, 2), (2, 2)], [(0, 2), (2, 2)], [(0, 2), (2, 1), (3, 1)], [(0, 2), (2, 1), (3, 1)]]
W_PIECES = [[(0, P)], [(0, P)], [(0, P // 2), (P // 2, P)], [(0, P // 2), (P // 2, P)]]
FIRST_S = [256, 256, 192, 160]
CUT = 224
HALF = S // 2
QUARTERS = [(0, 128), (128, 256), (256, 384), (384, 512)]
STORES = [(0, 64), (64, 128)]


def tile_picked_pool_lin_bias_sub_e_kernel(tc, xT, w_words, w_scales, b, offs, out):
    nc = tc.nc
    with ExitStack() as ctx:
        keep = ctx.enter_context(tc.tile_pool(name="keep", bufs=1))
        psum = ctx.enter_context(tc.psum_pool(name="psum", bufs=1))

        offsets = keep.tile([P, S // 16], U16, name="offsets")
        w_codes = [keep.tile([P, N], U32, name="w_codes_%d" % a, align_bytes=BURST) for a in range(PASSES)]
        w_plane = keep.tile([P, N], U8, name="w_plane", align_bytes=64)
        bias = keep.tile([P, 1], F32, name="bias")
        nc.gpsimd.memset(w_plane[:].bitcast(I32), 0)

        scale_words = w_scales.bitcast(I32)
        last = PASSES - 1

        x_rows = xT.rearrange("(a p t) n -> a p t n", p=P, t=PACK)
        w_rows = w_words.rearrange("a p m r -> a p (m r)").bitcast(I32)
        window = {}
        for a in range(PASSES):
            for t0, count in LOADS[a]:
                raw = keep.tile([P, count, T], F32, name="raw_%d_%d" % (a, t0), align_bytes=BURST)
                nc.sync.dma_start(raw[:], x_rows[a, :, t0 : t0 + count, :])
                for t in range(count):
                    window[a, t0 + t] = raw[:, t, :]
                if (a, t0) == (0, 0):
                    nc.sync.dma_start(offsets[:], offs)
                    for q in range(4):
                        nc.sync.dma_start(
                            w_plane[32 * q : 32 * q + 16, :].bitcast(I32), scale_words[:, 4 * q : 4 * q + 4, :]
                        )
        for a in range(PASSES):
            for p0, p1 in W_PIECES[a]:
                nc.sync.dma_start(w_codes[a][p0:p1, :].bitcast(I32), w_rows[a, p0:p1, :])
        nc.sync.dma_start(bias[:], b)

        pooled = keep.tile([P, V], F32, name="pooled")
        result = keep.tile([P, V], F32, name="result", align_bytes=BURST)
        picked = [keep.tile([P, PACK, S], F32, name="picked_%d" % a) for a in range(PASSES)]
        grouped = [keep.tile([P, PACK * S], BF16, name="grouped_%d" % a, align_bytes=64) for a in range(PASSES)]
        codes = [keep.tile([P, S], U32, name="codes_%d" % a, align_bytes=64) for a in range(PASSES)]
        planes = [keep.tile([P, S], U8, name="plane_%d" % a, align_bytes=64) for a in range(PASSES)]
        accs = [psum.tile([P, j1 - j0], F32, name="acc_%d" % j0) for j0, j1 in QUARTERS]

        def gather_v(a, t, j0, j1):
            nc.vector.tensor_copy(picked[a][:, t, j0:j1], window[a, t].indirect(offsets[:, j0 // 16 : j1 // 16]))

        def gather_s(a, t, j0, j1):
            nc.scalar.activation(picked[a][:, t, j0:j1], window[a, t].indirect(offsets[:, j0 // 16 : j1 // 16]), COPY)

        def weave(copy, a, j0, j1):
            copy(
                grouped[a][:, PACK * j0 : PACK * j1].rearrange("p (c i t) -> p c t i", i=LINE, t=PACK),
                picked[a][:, :, j0:j1].rearrange("p t (c i) -> p c t i", i=LINE),
            )

        def quantise(a, j0, j1):
            nc.vector.quantize_mx(
                out=codes[a][:, j0:j1].bitcast(FP8X4),
                scales=planes[a][:, j0:j1],
                in_=grouped[a][:, PACK * j0 : PACK * j1],
            )

        def multiply(a, g):
            j0, j1 = QUARTERS[g]
            nc.tensor.matmul_mx(
                out=accs[g][:],
                lhsT=w_codes[a][:].bitcast(FP8X4),
                lhsT_scale=w_plane[4 * a :, :],
                rhs=codes[a][:, j0:j1].bitcast(FP8X4),
                rhs_scale=planes[a][:, j0:j1],
                start=(a == 0),
                stop=(a == last),
            )

        for a in range(PASSES):
            if a == 0:
                gather_s(a, 1, 0, FIRST_S[a])
                gather_v(a, 0, 0, S)
            else:
                gather_s(a, 0, 0, S)
                gather_s(a, 1, 0, FIRST_S[a])
            gather_v(a, 1, FIRST_S[a], S)
            if a < last:
                if a < last - 1:
                    gather_s(a, 2, 0, HALF)
                    gather_v(a, 3, 0, HALF)
                    gather_s(a, 2, HALF, S)
                    gather_v(a, 3, HALF, S)
                else:
                    gather_v(a, 2, 0, CUT)
                    gather_s(a, 2, CUT, S)
                    gather_v(a, 3, 0, HALF)
                    gather_s(a, 3, HALF, S)
                weave(nc.scalar.copy, a, 384, S)
                weave(nc.vector.tensor_copy, a, 0, HALF)
                weave(nc.vector.tensor_copy, a, HALF, 384)
                quantise(a, 0, HALF)
                quantise(a, HALF, S)
        gather_v(last, 2, 0, HALF)
        gather_s(last, 2, HALF, S)
        gather_v(last, 3, *QUARTERS[3])
        gather_v(last, 3, *QUARTERS[2])
        gather_s(last, 3, *QUARTERS[0])
        gather_s(last, 3, *QUARTERS[1])
        for a in range(last):
            for g in range(len(QUARTERS)):
                multiply(a, g)
        weave(nc.scalar.copy, last, *QUARTERS[2])
        weave(nc.scalar.copy, last, 384, 448)
        weave(nc.vector.tensor_copy, last, *QUARTERS[0])
        weave(nc.vector.tensor_copy, last, *QUARTERS[1])
        weave(nc.vector.tensor_copy, last, 448, S)
        for g in range(len(QUARTERS)):
            quantise(last, *QUARTERS[g])
        for g in range(len(QUARTERS)):
            multiply(last, g)
        for g, (j0, j1) in enumerate(QUARTERS):
            nc.vector.tensor_reduce(
                pooled[:, j0 // D : j1 // D],
                accs[g][:].rearrange("p (v d) -> p v d", d=D),
                mybir.AxisListType.X,
                mybir.AluOpType.max,
            )
        for v0, v1 in STORES:
            if v1 < V:
                nc.scalar.activation(result[:, v0:v1], pooled[:, v0:v1], IDENTITY, bias=bias[:])
            else:
                nc.vector.tensor_scalar_add(result[:, v0:v1], pooled[:, v0:v1], bias[:])
            nc.sync.dma_start(out[:, v0:v1], result[:, v0:v1])
